import numpy as np, ml_dtypes
CORES = [2,3,42,43,82,83,122,123]
N = 8
import mx_ref
BF = ml_dtypes.bfloat16
def entries(a):
    return np.ascontiguousarray(a.T).reshape(-1)
def table(e):
    return np.ascontiguousarray(np.reshape(e, (-1, 16)).T).astype(np.int32)
def f(rng, *shape):
    return mx_ref.flush((rng.standard_normal(shape, dtype=np.float32) * np.exp2(rng.integers(-2, 3, shape[:-1] + (1,)))).astype(BF))
def wide(rng, *shape, cols=0):
    v = rng.standard_normal(shape, dtype=np.float32) * np.exp2(rng.integers(-12, 13, shape)).astype(np.float32)
    if cols: v *= np.repeat(np.exp2(rng.integers(-cols, cols + 1, shape[:-2] + (1, shape[-1] // 4))) * (rng.random(shape[:-2] + (1, shape[-1] // 4)) > 0.0625), 4, axis=-1).astype(np.float32)
    return mx_ref.flush(v.astype(BF))
T = 512
def listed(a):
    k = np.full((2 * N, 128), -1)
    for s in range(2 * N):
        i = np.flatnonzero(a == s); k[s, :len(i)] = i
    return k.reshape(-1)
def lists(rng, one=False, absent=False, sort=False, alike=False):
    t, a, k = [], [], []; nobody = rng.integers(0, N)
    for r in range(N):
        if r == 0 or not alike:
            u = np.concatenate([rng.permutation(8)[:2] for q in range(N)])
            if absent:
                here = rng.permutation([q for q in range(N) if q != nobody])[:T // 256 + r % 3].tolist()
                u.reshape(N, 2)[[q for q in range(N) if q not in here]] = -1
            else: u[rng.permutation(2 * N)[:rng.integers(0, 5)]] = -1
        v = rng.permutation(np.flatnonzero(u >= 0))
        if one: e = np.concatenate([np.full(128, v[0]), np.resize(v[1:], T - 128)])
        else:
            room = np.zeros(2 * N, int); room[v] = rng.integers(0, 129, len(v))
            for s in v:
                if room.sum() < T: room[s] = 128
            e = np.repeat(np.arange(2 * N), room)
        e = rng.permutation(e)[:T]
        if sort: e = np.sort(e)
        t.append(table(u)); a.append(table(e)); k.append(table(listed(e)))
    return {"tab": np.stack(t), "ad": np.stack(a), "tok": np.stack(k)}
def setup_inputs(rng):
    return {"x": f(rng, N, 128, 4 * T), "wa": f(rng, N, 1024, 512), **lists(rng)}
def setup_inputs_absent(rng):
    return {**setup_inputs(rng), **lists(rng, absent=True)}
def setup_inputs_alike(rng):
    return {**setup_inputs(rng), **lists(rng, alike=True)}
def setup_inputs_one(rng):
    return {**setup_inputs(rng), **lists(rng, one=True)}
def setup_inputs_sorted(rng):
    return {**setup_inputs(rng), **lists(rng, sort=True)}
def setup_inputs_spread(rng):
    d = setup_inputs(rng); d["x"] = wide(rng, N, 128, 4 * T, cols=8); return d
def check_inputs(d):
    b = []
    for n in ("x", "wa"):
        v = np.abs(np.asarray(d[n]).astype(np.float32))
        if not ((v == 0) | ((v >= 2.0 ** -30) & (v <= 2.0 ** 30))).all(): b.append(n)
    for r in range(N):
        u, a, k = entries(d["tab"][r]), entries(d["ad"][r]), entries(d["tok"][r]); p = u.reshape(N, 2)
        if u.min() < -1 or u.max() > 7 or ((p[:, 0] == p[:, 1]) & (p[:, 0] >= 0)).any(): b.append("tab")
        if a.min() < 0 or a.max() >= 2 * N or (u[a] < 0).any() or np.bincount(a).max() > 128: b.append("ad")
        elif (k != listed(a)).any(): b.append("tok")
    return b
def reference(x, wa, tab, ad, tok):
    y = np.zeros((N, 128, T), np.float32)
    for r in range(N):
        u, a, X = entries(tab[r]), entries(ad[r]), mx_ref.quantize(x[r])
        for s in range(2 * N):
            i = np.flatnonzero(a == s)
            if len(i) == 0: continue
            A = wa[s // 2][128 * u[s]:128 * u[s] + 128]
            y[r][:, i] = mx_ref.matmul(mx_ref.quantize(A), X)[:, i]
    return {"y": y}

@@ -1,0 +1,352 @@
+from concourse.bass import DstId, RemoteDMATransfer
+from concourse.mybir import dt, AluOpType as Op, ActivationFunctionType as Fn
+
+NB = 10
+NC = 128 * NB
+NAT = 6
+W0 = 512 * NAT
+SPLIT = 608
+PW = 1824
+
+SCRATCH = {
+    "tab1": ("sbuf", [128, 16], "int32"),
+    "tabb": ("sbuf", [128, 16], "int32"),
+    "tabf": ("sbuf", [128, 16], "bfloat16"),
+    "tabl": ("sbuf", [128, 16], "bfloat16"),
+    "win": ("sbuf", [128, 4096], "bfloat16"),
+    "xs": ("sbuf", [128, 2048], "bfloat16"),
+    "xg": ("sbuf", [128, 4 * NC], "bfloat16"),
+    "ga": ("sbuf", [128, 8192], "bfloat16"),
+    "offa": ("sbuf", [128, 512], "uint16"),
+    "tokS": ("sbuf", [128, 80], "int32"),
+    "adS": ("sbuf", [128, 32], "int32"),
+    "offx": ("sbuf", [128, 80], "uint16"),
+    "offs": ("sbuf", [128, 80], "uint16"),
+    "offy": ("sbuf", [128, 32], "uint16"),
+    "pidx": ("sbuf", [128, 4], "int32"),
+    "pi1": ("sbuf", [128, 4], "int32"),
+    "pi2": ("sbuf", [128, 4], "int32"),
+    "p16f": ("sbuf", [128, 4], "float32"),
+    "oddf": ("sbuf", [128, 4], "float32"),
+    "evf": ("sbuf", [128, 4], "float32"),
+    "odd16": ("sbuf", [128, 4], "float32"),
+    "iot": ("sbuf", [128, 80], "float32"),
+    "dumpc": ("sbuf", [128, 80], "float32"),
+    "tokA": ("sbuf", [128, 80], "int32"),
+    "tokB": ("sbuf", [128, 80], "int32"),
+    "negf": ("sbuf", [128, 80], "float32"),
+    "ndf": ("sbuf", [128, 80], "float32"),
+    "offf": ("sbuf", [128, 80], "float32"),
+    "ones": ("sbuf", [128, NC], "float32"),
+    "vals": ("sbuf", [128, NC], "float32"),
+    "posw": ("sbuf", [128, PW], "float32"),
+    "trp": ("sbuf", [128, 512], "float32"),
+    "f1": ("sbuf", [128, 32], "float32"),
+    "f2": ("sbuf", [128, 32], "float32"),
+    "f3": ("sbuf", [128, 32], "float32"),
+    "n1": ("sbuf", [128, 32], "float32"),
+    "n2": ("sbuf", [128, 32], "float32"),
+    "n3": ("sbuf", [128, 32], "float32"),
+    "n4": ("sbuf", [128, 32], "float32"),
+    "tot": ("sbuf", [128, 32], "float32"),
+    "qc": ("sbuf", [128, 2048], "float8_e4m3fn_x4"),
+    "qs": ("sbuf", [128, 2048], "uint8"),
+    "lc": ("sbuf", [128, 2048], "float8_e4m3fn_x4"),
+    "ls": ("sbuf", [128, 2048], "uint8"),
+    "xc": ("sbuf", [128, 512], "float8_e4m3fn_x4"),
+    "xcs": ("sbuf", [128, 512], "uint8"),
+    "xgc": ("sbuf", [128, NC], "float8_e4m3fn_x4"),
+    "xgs": ("sbuf", [128, NC], "uint8"),
+    "resw": ("sbuf", [128, W0 + NC], "float32"),
+    "ysb": ("sbuf", [128, 512], "float32"),
+}
+for _b in range(8):
+    SCRATCH["ps%d" % _b] = ("psum", [128, 512], "float32")
+NEV = 118
+SEMAPHORES = (["e%d" % _i for _i in range(NEV)] + ["a%d" % _i for _i in range(8)]
+              + ["dtab", "dx", "dw", "dt", "da", "dy0", "dy1", "tsent", "tabs", "loc", "ha", "hb"])
+
+
+def _mask(es):
+    return sum(1 << e for e in es)
+
+
+def _road(r, T, topo):
+    cores = list(T.cores)
+    chips = []
+    for c in cores:
+        if topo.chip(c) not in chips:
+            chips.append(topo.chip(c))
+    mem = [[q for q in range(len(cores)) if topo.chip(cores[q]) == ch] for ch in chips]
+    me = cores[r]
+    k = chips.index(topo.chip(me))
+    h = mem[k].index(r)
+    rel = [mem[k ^ s][1 - h] for s in (1, 2, 3)]
+    dire = [mem[k ^ s][h] for s in (1, 2, 3)]
+    nb = mem[k][1 - h]
+    helper = [c for c in topo.cores_of(me) if topo.die(c) != topo.die(me)
+              and all(topo.may_write(c, cores[d]) for d in rel)][h]
+    off = topo.engines(me, cores[dire[0]])
+    on = [e for e in topo.engines(me, cores[nb]) if e not in off]
+    hoff = topo.engines(helper, cores[rel[0]])
+    H = len(off) // 2
+    eng = {rel[0]: hoff[:H], rel[1]: hoff[H:], rel[2]: hoff,
+           dire[0]: off, dire[1]: off[:H], dire[2]: off[H:], nb: on}
+    tabe, left = {}, list(off)
+    for i, d in enumerate(rel + dire):
+        n = 2 if i < len(off) - len(rel + dire) else 1
+        tabe[d], left = left[:n], left[n:]
+    tabe[nb] = on
+    return {"k": k, "h": h, "rel": rel, "dir": dire, "nb": nb, "helper": helper, "off": off, "on": on,
+            "eng": eng, "tab": tabe, "pairs": rel + dire + [nb, r], "mem": mem}
+
+
+def _tr(topo, dst, engines, sem, src, to):
+    rid, pid, _se = topo.addr(dst)
+    return RemoteDMATransfer(dst_ids=[DstId(rid=rid, pnc=pid)], dma_engine_mask=_mask(engines), remote_sem=sem, src=src, dst=to)
+
+
+def _codes(buf, a, b):
+    return buf[:, a:b].bitcast(dt.uint8)
+
+
+def _relay(g, r, R, T, topo):
+    cores = list(T.cores)
+    n = [0]
+
+    def send(items):
+        for c, buf in ((True, "lc"), (False, "ls")):
+            ts = []
+            for a, d in items:
+                s, t = T[buf], T[buf]
+                src = _codes(s, a, a + 256) if c else s[:, a:a + 256]
+                dst = _codes(t, 256 * r, 256 * r + 256) if c else t[:, 256 * r:256 * r + 256]
+                ts.append(_tr(topo, cores[d], R["eng"][d], T.sem["a%d" % r], src, dst))
+                n[0] += len(R["eng"][d])
+            g.remote_dma_fused(ts, local_sem=T.sem.loc)
+
+    every = len(topo.engines(cores[r], R["helper"]))
+    g.wait_ge(T.sem.ha, 2 * every)
+    send([(0, R["rel"][0]), (256, R["rel"][1])])
+    g.wait_ge(T.sem.hb, 2 * len(R["on"]))
+    send([(512, R["rel"][2])])
+    g.wait_ge(T.sem.loc, n[0])
+
+
+def rank_program(g, core, T, topo):
+    rank = T.rank_of(core)
+    cores = list(T.cores)
+    roads = [_road(q, T, topo) for q in range(len(cores))]
+    if rank is None:
+        for q, R in enumerate(roads):
+            if R["helper"] == core:
+                _relay(g, q, R, T, topo)
+        return
+    R = roads[rank]
+    V, S, P, Y = g.vector, g.scalar, g.tensor, g.sync
+    pairs = R["pairs"]
+    nat0 = 0 if R["k"] < 2 else 16 - NAT
+    listed = [s for s in range(16) if not nat0 <= s < nat0 + NAT]
+    c0 = 8 * listed[0]
+    used = [0]
+    waited = {}
+
+    def new():
+        used[0] += 1
+        return ["e%d" % (used[0] - 1), 0]
+
+    def sig(inst, e=None):
+        e = e or new()
+        inst.then_inc(T.sem[e[0]], 1)
+        e[1] += 1
+        return e
+
+    def need(qn, *es):
+        q = {"g": g, "V": V, "S": S, "P": P, "Y": Y}[qn]
+        for e in es:
+            if waited.get((qn, e[0]), 0) < e[1]:
+                q.wait_ge(T.sem[e[0]], e[1])
+                waited[(qn, e[0])] = e[1]
+
+    Y.dma_start(T.tab1[0:1, 0:16], T.tab[:]).then_inc(T.sem.dtab, 16)
+    for b in range(8):
+        S.dma_start(T.tokS[16 * b:16 * b + 16, :], T.tok[:, c0:c0 + 80]).then_inc(T.sem.dt, 16)
+    Y.dma_start(T.xs[:], T.x[:]).then_inc(T.sem.dx, 16)
+    for m in range(8):
+        if m == 2:
+            Y.wait_ge(T.sem.tsent, 1)
+        Y.dma_start(T.win[:, 512 * m:512 * m + 512], T.wa[128 * m:128 * m + 128, :]).then_inc(T.sem.dw, 16)
+    for b in range(8):
+        S.dma_start(T.adS[16 * b:16 * b + 16, :], T.ad[:]).then_inc(T.sem.da, 16)
+
+    e_pidx = sig(g.iota(T.pidx[:, 0:1], [[0, 1]], 0, 1))
+    e_iot = sig(g.iota(T.iot[:], [[16, 80]], 17, 0, allow_small_or_imprecise_dtypes=True))
+    g.wait_ge(T.sem.dtab, 16)
+    e_pb = sig(g.partition_broadcast(T.tabb[:], T.tab1[0:1, 0:16], 128))
+
+    need("V", e_pidx)
+    e1 = sig(V.tensor_scalar(T.pi1[:, 0:1], T.pidx[:, 0:1], 15, None, Op.bitwise_and))
+    e2 = sig(V.tensor_scalar(T.pi2[:, 0:1], T.pidx[:, 0:1], 4, 1, Op.logical_shift_right, Op.bitwise_and))
+    need("V", e1, e2)
+    e_p16 = sig(V.tensor_copy(T.p16f[:, 0:1], T.pi1[:, 0:1]))
+    e_c = sig(V.tensor_copy(T.oddf[:, 0:1], T.pi2[:, 0:1]))
+    sig(V.tensor_scalar(T.odd16[:, 0:1], T.pi2[:, 0:1], 16.0, None, Op.mult), e_c)
+    sig(V.tensor_scalar(T.evf[:, 0:1], T.pi2[:, 0:1], -1.0, 1.0, Op.mult, Op.add), e_c)
+    need("V", e_iot, e_p16)
+    sig(V.tensor_scalar(T.dumpc[:], T.iot[:], T.p16f[:, 0:1], None, Op.add), e_c)
+    e_one = sig(V.memset(T.ones[:], 1.0))
+    e_pz = sig(V.memset(T.posw[:, 0:512], 0.0))
+    need("V", e_pb)
+    e_tab = sig(V.tensor_scalar(T.tabf[:], T.tabb[:], 0.0, 512.0, Op.max, Op.mult))
+
+    need("g", e_tab)
+    g.remote_dma_fused([_tr(topo, cores[d], R["tab"][d], T.sem.tabs, T.tabf[:, 2 * d:2 * d + 2],
+                            T.tabl[:, 2 * rank:2 * rank + 2]) for d in pairs[:7]], local_sem=T.sem.loc)
+    nloc = sum(len(R["tab"][d]) for d in pairs[:7])
+    g.sem_inc(T.sem.tsent, 1)
+
+    V.wait_ge(T.sem.dt, 128)
+    e_ox = sig(V.tensor_scalar(T.offx[:], T.tokS[:], 0.0, 4.0, Op.max, Op.mult))
+    need("V", e_one, e_c)
+    e_val = sig(V.tensor_tensor_scan(T.vals[:], T.ones[:], T.ones[:], float(W0 - 1), Op.mult, Op.add))
+    e3 = sig(V.tensor_scalar(T.tokA[:], T.tokS[:], T.odd16[:, 0:1], None, Op.subtract))
+    e4 = sig(V.tensor_scalar(T.negf[:], T.tokS[:], 0.0, None, Op.is_lt))
+    need("V", e3)
+    e5 = sig(V.tensor_scalar(T.tokB[:], T.tokA[:], 511, None, Op.bitwise_and))
+    need("V", e4)
+    e6 = sig(V.tensor_tensor(T.ndf[:], T.negf[:], T.dumpc[:], Op.mult))
+    need("V", e5, e6)
+    e7 = sig(V.tensor_tensor(T.offf[:], T.ndf[:], T.tokB[:], Op.add))
+    need("V", e7)
+    e8 = sig(V.tensor_copy(T.offs[:], T.offf[:]))
+    need("V", e8, e_val, e_pz)
+    e_sc = sig(V.tensor_copy(T.posw[:].indirect(T.offs[:]), T.vals[:]))
+    V.wait_ge(T.sem.dx, 16)
+    e_xq = sig(V.quantize_mx(T.xc[:], T.xcs[:], T.xs[:]))
+
+    e_xg = new()
+
+    def xgather(t):
+        sig(S.activation(T.xg[:, t:4 * NC:4], T.xs[:, t:2048].indirect(T.offx[:]), Fn.Copy), e_xg)
+
+    S.wait_ge(T.sem.dx, 16)
+    need("S", e_ox)
+    for t in range(3):
+        xgather(t)
+
+    V.wait_ge(T.sem.tabs, sum(len(roads[q]["tab"][rank]) for q in range(len(cores)) if q != rank))
+    e_off = []
+    for i, d in enumerate(pairs):
+        t, e = (T.tabf if d == rank else T.tabl), new()
+        for j in range(2):
+            sig(V.tensor_scalar(T.offa[:, 64 * i + 32 * j:64 * i + 32 * j + 32], T.dumpc[:, 0:32],
+                                t[:, 2 * (rank if d == rank else d) + j:2 * (rank if d == rank else d) + j + 1]
+                                if d != rank else t[:, 2 * rank + j:2 * rank + j + 1], -17.0, Op.add, Op.add), e)
+        e_off.append(e)
+
+    V.wait_ge(T.sem.dw, 128)
+    S.wait_ge(T.sem.dw, 128)
+    e_q = []
+    for i in range(8):
+        a, m = 1024 * i, SPLIT // 16
+        need("S", e_off[i])
+        es = sig(S.activation(T.ga[:, a:a + SPLIT], T.win[:].indirect(T.offa[:, 64 * i:64 * i + m]), Fn.Copy))
+        need("V", e_off[i])
+        ev = sig(V.tensor_copy(T.ga[:, a + SPLIT:a + 1024], T.win[:].indirect(T.offa[:, 64 * i + m:64 * i + 64])))
+        need("V", es, ev)
+        e_q.append(sig(V.quantize_mx(T.qc[:, 256 * i:256 * i + 256], T.qs[:, 256 * i:256 * i + 256], T.ga[:, a:a + 1024])))
+    xgather(3)
+
+    def send(items):
+        n = 0
+        for c, (b, l) in ((True, ("qc", "lc")), (False, ("qs", "ls"))):
+            ts = []
+            for i, w, dst, engines, sem, at in items:
+                src = _codes(T[b], 256 * i, 256 * i + w) if c else T[b][:, 256 * i:256 * i + w]
+                to = _codes(T[l], at, at + w) if c else T[l][:, at:at + w]
+                ts.append(_tr(topo, dst, engines, sem, src, to))
+                n += len(engines)
+            g.remote_dma_fused(ts, local_sem=T.sem.loc)
+        return n
+
+    mine = T.sem["a%d" % rank]
+    need("g", e_q[0], e_q[1])
+    nloc += send([(0, 512, R["helper"], topo.engines(core, R["helper"]), T.sem.ha, 0)])
+    need("g", e_q[2], e_q[3])
+    nloc += send([(2, 256, R["helper"], R["on"], T.sem.hb, 512),
+                  (3, 256, cores[R["dir"][0]], R["eng"][R["dir"][0]], mine, 256 * rank)])
+    need("g", e_q[4], e_q[5])
+    nloc += send([(i, 256, cores[R["dir"][i - 3]], R["eng"][R["dir"][i - 3]], mine, 256 * rank) for i in (4, 5)])
+    need("g", e_q[6])
+    nloc += send([(6, 256, cores[R["nb"]], R["eng"][R["nb"]], mine, 256 * rank)])
+    g.wait_ge(T.sem.loc, nloc)
+
+    need("V", e_sc)
+    e_t = sig(V.transpose(T.trp[:], T.posw[:, 0:512]))
+    V.wait_ge(T.sem.da, 128)
+    if nat0 == 0:
+        n1 = sig(V.tensor_scalar(T.n1[:], T.adS[:], NAT - 0.5, None, Op.is_lt))
+    else:
+        n1 = sig(V.tensor_scalar(T.n1[:], T.adS[:], nat0 - 0.5, None, Op.is_gt))
+    n2 = sig(V.tensor_scalar(T.n2[:], T.adS[:], 512.0, -512.0 * nat0 - 17.0, Op.mult, Op.add))
+    need("V", e_t)
+    f = sig(V.tensor_scalar(T.f1[:], T.trp[:, 0:512:16], T.evf[:, 0:1], None, Op.mult))
+    sig(V.tensor_scalar(T.f2[:, 1:32], T.trp[:, 0:496:16], T.oddf[:, 0:1], None, Op.mult), f)
+    sig(V.tensor_scalar(T.f2[:, 0:1], T.trp[:, 496:497], T.oddf[:, 0:1], None, Op.mult), f)
+    need("V", n2)
+    n3 = sig(V.tensor_tensor(T.n3[:], T.n2[:], T.dumpc[:, 0:32], Op.add))
+    need("V", f)
+    f3 = sig(V.tensor_tensor(T.f3[:], T.f1[:], T.f2[:], Op.add))
+    need("V", n1, n3)
+    n4 = sig(V.tensor_tensor(T.n4[:], T.n3[:], T.n1[:], Op.mult))
+    need("V", n4, f3)
+    tt = sig(V.tensor_tensor(T.tot[:], T.n4[:], T.f3[:], Op.add))
+    need("V", tt)
+    e_oy = sig(V.tensor_copy(T.offy[:], T.tot[:]))
+    need("V", e_xg)
+    e_gq = []
+    for a, b in ((0, 512), (512, 1024), (1024, NC)):
+        e_gq.append(sig(V.quantize_mx(T.xgc[:, a:b], T.xgs[:, a:b], T.xg[:, 4 * a:4 * b])))
+
+    k, h, mem = R["k"], R["h"], R["mem"]
+    order = [rank, R["nb"], mem[k ^ 1][1 - h], mem[k ^ 1][h], mem[k ^ 2][1 - h], mem[k ^ 3][1 - h], mem[k ^ 2][h], mem[k ^ 3][h]]
+    copies, n = [], 0
+    for src in order:
+        if src == rank:
+            need("P", e_q[7])
+            cb, sb, at = T.qc, T.qs, 256 * 7
+        else:
+            P.wait_ge(T.sem["a%d" % src], 2 * len(roads[src]["eng"][rank]))
+            cb, sb, at = T.lc, T.ls, 256 * src
+        for j in range(2):
+            s, b = 2 * src + j, T["ps%d" % (n % 8)]
+            if n >= 8:
+                need("P", copies[n - 8])
+            if s in listed:
+                x0, w, xa, xb = 128 * listed.index(s), 128, T.xgc, T.xgs
+                need("P", e_gq[x0 // 512])
+                out = W0 + x0
+            else:
+                x0, w, xa, xb = 0, 512, T.xc, T.xcs
+                need("P", e_xq)
+                out = 512 * (s - nat0)
+            e = sig(P.matmul_mx(b[:, 0:w], cb[:, at + 128 * j:at + 128 * j + 128], sb[:, at + 128 * j:at + 128 * j + 128],
+                                xa[:, x0:x0 + w], xb[:, x0:x0 + w], True, True))
+            if j == 0:
+                need("S", e)
+                copies.append(sig(S.activation(T.resw[:, out:out + w], b[:, 0:w], Fn.Copy)))
+            else:
+                need("V", e)
+                copies.append(sig(V.tensor_copy(T.resw[:, out:out + w], b[:, 0:w])))
+            n += 1
+
+    need("V", e_oy, *copies)
+    e_y = sig(V.tensor_copy(T.ysb[:, 0:256], T.resw[:].indirect(T.offy[:, 0:16])))
+    need("S", e_oy, *copies)
+    e_z = sig(S.activation(T.ysb[:, 256:512], T.resw[:].indirect(T.offy[:, 16:32]), Fn.Copy))
+    need("Y", e_y)
+    Y.dma_start(T.y[:, 0:256], T.ysb[:, 0:256]).then_inc(T.sem.dy0, 16)
+    need("S", e_z)
+    S.dma_start(T.y[:, 256:512], T.ysb[:, 256:512]).then_inc(T.sem.dy1, 16)
+    Y.wait_ge(T.sem.dy0, 16)
+    S.wait_ge(T.sem.dy1, 16)

@@ -5,66 +5,27 @@ NB = 10
 NC = 128 * NB
 NAT = 6
 W0 = 512 * NAT
-SPLIT = 608
+SPLIT = 640
+XE = 2
+SE = 960
 PW = 1824
 
-SCRATCH = {
-    "tab1": ("sbuf", [128, 16], "int32"),
-    "tabb": ("sbuf", [128, 16], "int32"),
-    "tabf": ("sbuf", [128, 16], "bfloat16"),
-    "tabl": ("sbuf", [128, 16], "bfloat16"),
-    "win": ("sbuf", [128, 4096], "bfloat16"),
-    "xs": ("sbuf", [128, 2048], "bfloat16"),
-    "xg": ("sbuf", [128, 4 * NC], "bfloat16"),
-    "ga": ("sbuf", [128, 8192], "bfloat16"),
-    "offa": ("sbuf", [128, 512], "uint16"),
-    "tokS": ("sbuf", [128, 80], "int32"),
-    "adS": ("sbuf", [128, 32], "int32"),
-    "offx": ("sbuf", [128, 80], "uint16"),
-    "offs": ("sbuf", [128, 80], "uint16"),
-    "offy": ("sbuf", [128, 32], "uint16"),
-    "pidx": ("sbuf", [128, 4], "int32"),
-    "pi1": ("sbuf", [128, 4], "int32"),
-    "pi2": ("sbuf", [128, 4], "int32"),
-    "p16f": ("sbuf", [128, 4], "float32"),
-    "oddf": ("sbuf", [128, 4], "float32"),
-    "evf": ("sbuf", [128, 4], "float32"),
-    "odd16": ("sbuf", [128, 4], "float32"),
-    "iot": ("sbuf", [128, 80], "float32"),
-    "dumpc": ("sbuf", [128, 80], "float32"),
-    "tokA": ("sbuf", [128, 80], "int32"),
-    "tokB": ("sbuf", [128, 80], "int32"),
-    "negf": ("sbuf", [128, 80], "float32"),
-    "ndf": ("sbuf", [128, 80], "float32"),
-    "offf": ("sbuf", [128, 80], "float32"),
-    "ones": ("sbuf", [128, NC], "float32"),
-    "vals": ("sbuf", [128, NC], "float32"),
-    "posw": ("sbuf", [128, PW], "float32"),
-    "trp": ("sbuf", [128, 512], "float32"),
-    "f1": ("sbuf", [128, 32], "float32"),
-    "f2": ("sbuf", [128, 32], "float32"),
-    "f3": ("sbuf", [128, 32], "float32"),
-    "n1": ("sbuf", [128, 32], "float32"),
-    "n2": ("sbuf", [128, 32], "float32"),
-    "n3": ("sbuf", [128, 32], "float32"),
-    "n4": ("sbuf", [128, 32], "float32"),
-    "tot": ("sbuf", [128, 32], "float32"),
-    "qc": ("sbuf", [128, 2048], "float8_e4m3fn_x4"),
-    "qs": ("sbuf", [128, 2048], "uint8"),
-    "lc": ("sbuf", [128, 2048], "float8_e4m3fn_x4"),
-    "ls": ("sbuf", [128, 2048], "uint8"),
-    "xc": ("sbuf", [128, 512], "float8_e4m3fn_x4"),
-    "xcs": ("sbuf", [128, 512], "uint8"),
-    "xgc": ("sbuf", [128, NC], "float8_e4m3fn_x4"),
-    "xgs": ("sbuf", [128, NC], "uint8"),
-    "resw": ("sbuf", [128, W0 + NC], "float32"),
-    "ysb": ("sbuf", [128, 512], "float32"),
-}
+SCRATCH = {n: ("sbuf", [128, w], d) for d, ws in {
+    "int32": {"tab1": 16, "tabb": 16, "tokS": 80, "adS": 32, "pidx": 4, "pi1": 4, "pi2": 4, "tokA": 80, "tokB": 80},
+    "bfloat16": {"tabf": 16, "win": 4096, "xs": 2048, "xg": 4 * NC, "ga": 8192},
+    "uint16": {"offa": 512, "offx": 80, "offs": 80, "offy": 32},
+    "float32": {"p16f": 4, "oddf": 4, "evf": 4, "odd16": 4, "iot": 80, "dumpc": 80, "negf": 80, "ndf": 80, "offf": 80,
+                "vals": NC, "posw": PW, "trp": 512, "f1": 32, "f2": 32, "f3": 32, "n1": 32, "n2": 32, "n3": 32, "n4": 32,
+                "tot": 32, "resw": W0 + NC, "ysb": 512},
+    "float8_e4m3fn_x4": {"qc": 2048, "lc": 2048, "xc": 512, "xgc": NC},
+    "uint8": {"qs": 2048, "ls": 2048, "xcs": 512, "xgs": NC},
+}.items() for n, w in ws.items()}
+SCRATCH["tabd"] = ("dram", [128, 1], "int32")
+SCRATCH["tabr"] = ("dram", [8, 128, 1], "int32")
 for _b in range(8):
     SCRATCH["ps%d" % _b] = ("psum", [128, 512], "float32")
-NEV = 118
-SEMAPHORES = (["e%d" % _i for _i in range(NEV)] + ["a%d" % _i for _i in range(8)]
-              + ["dtab", "dx", "dw", "dt", "da", "dy0", "dy1", "tsent", "tabs", "loc", "ha", "hb"])
+SEMAPHORES = (["e%d" % _i for _i in range(120)] + ["a%d" % _i for _i in range(8)]
+              + ["dtab", "dtw", "dx", "dw", "dt", "da", "dy0", "dy1", "tabs", "tsent", "loc", "h0", "h1"])
 
 
 def _mask(es):
@@ -84,21 +45,23 @@ def _road(r, T, topo):
     rel = [mem[k ^ s][1 - h] for s in (1, 2, 3)]
     dire = [mem[k ^ s][h] for s in (1, 2, 3)]
     nb = mem[k][1 - h]
-    helper = [c for c in topo.cores_of(me) if topo.die(c) != topo.die(me)
-              and all(topo.may_write(c, cores[d]) for d in rel)][h]
+    free = [c for c in topo.cores_of(me) if c not in cores]
+    port = [c for c in free if topo.die(c) != topo.die(me) and all(topo.may_write(c, cores[d]) for d in rel)]
+    far = [c for c in free if topo.die(c) != topo.die(me) and c not in port and topo.may_write(c, cores[rel[1]])]
+    near = [c for c in free if topo.die(c) == topo.die(me) and topo.may_write(c, cores[dire[1]])]
+    via = {rel[0]: port[h], rel[2]: port[h], rel[1]: far[h], dire[1]: near[h]}
     off = topo.engines(me, cores[dire[0]])
     on = [e for e in topo.engines(me, cores[nb]) if e not in off]
-    hoff = topo.engines(helper, cores[rel[0]])
-    H = len(off) // 2
-    eng = {rel[0]: hoff[:H], rel[1]: hoff[H:], rel[2]: hoff,
-           dire[0]: off, dire[1]: off[:H], dire[2]: off[H:], nb: on}
+    eng = {d: topo.engines(via.get(d, me), cores[d]) for d in rel + dire}
+    eng[nb] = on
     tabe, left = {}, list(off)
     for i, d in enumerate(rel + dire):
         n = 2 if i < len(off) - len(rel + dire) else 1
         tabe[d], left = left[:n], left[n:]
     tabe[nb] = on
-    return {"k": k, "h": h, "rel": rel, "dir": dire, "nb": nb, "helper": helper, "off": off, "on": on,
-            "eng": eng, "tab": tabe, "pairs": rel + dire + [nb, r], "mem": mem}
+    pairs = [rel[0], rel[1], dire[1], dire[0], rel[2], dire[2], nb, r]
+    return {"k": k, "h": h, "nb": nb, "via": via, "off": off, "on": on, "eng": eng, "tab": tabe, "pairs": pairs,
+            "order": [r, nb, rel[0], rel[1], dire[0], dire[1], rel[2], dire[2]]}
 
 
 def _tr(topo, dst, engines, sem, src, to):
@@ -106,31 +69,27 @@ def _tr(topo, dst, engines, sem, src, to):
     return RemoteDMATransfer(dst_ids=[DstId(rid=rid, pnc=pid)], dma_engine_mask=_mask(engines), remote_sem=sem, src=src, dst=to)
 
 
-def _codes(buf, a, b):
-    return buf[:, a:b].bitcast(dt.uint8)
+def _send(g, T, topo, bufs, items):
+    n = 0
+    for c, (b, l) in zip((True, False), bufs):
+        ts = []
+        for a, w, dst, engines, sem, at in items:
+            src, to = T[b][:, a:a + w], T[l][:, at:at + w]
+            ts.append(_tr(topo, dst, engines, sem, src.bitcast(dt.uint8) if c else src, to.bitcast(dt.uint8) if c else to))
+            n += len(engines)
+        g.remote_dma_fused(ts, local_sem=T.sem.loc)
+    return n
 
 
-def _relay(g, r, R, T, topo):
-    cores = list(T.cores)
-    n = [0]
-
-    def send(items):
-        for c, buf in ((True, "lc"), (False, "ls")):
-            ts = []
-            for a, d in items:
-                s, t = T[buf], T[buf]
-                src = _codes(s, a, a + 256) if c else s[:, a:a + 256]
-                dst = _codes(t, 256 * r, 256 * r + 256) if c else t[:, 256 * r:256 * r + 256]
-                ts.append(_tr(topo, cores[d], R["eng"][d], T.sem["a%d" % r], src, dst))
-                n[0] += len(R["eng"][d])
-            g.remote_dma_fused(ts, local_sem=T.sem.loc)
-
-    every = len(topo.engines(cores[r], R["helper"]))
-    g.wait_ge(T.sem.ha, 2 * every)
-    send([(0, R["rel"][0]), (256, R["rel"][1])])
-    g.wait_ge(T.sem.hb, 2 * len(R["on"]))
-    send([(512, R["rel"][2])])
-    g.wait_ge(T.sem.loc, n[0])
+def _relay(g, core, r, R, T, topo):
+    n, i = 0, 0
+    for d in R["pairs"]:
+        if R["via"].get(d) == core:
+            g.wait_ge(T.sem["h%d" % i], 2 * len(R["on"]))
+            n += _send(g, T, topo, (("lc", "lc"), ("ls", "ls")),
+                       [(256 * i, 256, T.cores[d], R["eng"][d], T.sem["a%d" % r], 256 * r)])
+            i += 1
+    g.wait_ge(T.sem.loc, n)
 
 
 def rank_program(g, core, T, topo):
@@ -139,8 +98,8 @@ def rank_program(g, core, T, topo):
     roads = [_road(q, T, topo) for q in range(len(cores))]
     if rank is None:
         for q, R in enumerate(roads):
-            if R["helper"] == core:
-                _relay(g, q, R, T, topo)
+            if core in R["via"].values():
+                _relay(g, core, q, R, T, topo)
         return
     R = roads[rank]
     V, S, P, Y = g.vector, g.scalar, g.tensor, g.sync
@@ -168,20 +127,36 @@ def rank_program(g, core, T, topo):
                 q.wait_ge(T.sem[e[0]], e[1])
                 waited[(qn, e[0])] = e[1]
 
-    Y.dma_start(T.tab1[0:1, 0:16], T.tab[:]).then_inc(T.sem.dtab, 16)
+    Y.dma_start(T.tabd[0:16, :], T.tab[:]).then_inc(T.sem.dtab, 16)
+    S.dma_start(T.tabd[16:128, :], T.tok[0:7, 0:16]).then_inc(T.sem.dtab, 16)
+    S.dma_start(T.tabr[rank, 0:16, :], T.tab[:]).then_inc(T.sem.dtab, 16)
     for b in range(8):
-        S.dma_start(T.tokS[16 * b:16 * b + 16, :], T.tok[:, c0:c0 + 80]).then_inc(T.sem.dt, 16)
+        (S if b < 4 else Y).dma_start(T.tokS[16 * b:16 * b + 16, :], T.tok[:, c0:c0 + 80]).then_inc(T.sem.dt, 16)
     Y.dma_start(T.xs[:], T.x[:]).then_inc(T.sem.dx, 16)
     for m in range(8):
-        if m == 2:
+        if m == 4:
             Y.wait_ge(T.sem.tsent, 1)
         Y.dma_start(T.win[:, 512 * m:512 * m + 512], T.wa[128 * m:128 * m + 128, :]).then_inc(T.sem.dw, 16)
     for b in range(8):
-        S.dma_start(T.adS[16 * b:16 * b + 16, :], T.ad[:]).then_inc(T.sem.da, 16)
+        Y.dma_start(T.adS[16 * b:16 * b + 16, :], T.ad[:]).then_inc(T.sem.da, 16)
 
     e_pidx = sig(g.iota(T.pidx[:, 0:1], [[0, 1]], 0, 1))
     e_iot = sig(g.iota(T.iot[:], [[16, 80]], 17, 0, allow_small_or_imprecise_dtypes=True))
-    g.wait_ge(T.sem.dtab, 16)
+    e_v0 = sig(g.iota(T.vals[:, 0:512], [[1, 512]], W0, 0, allow_small_or_imprecise_dtypes=True))
+    need("S", e_v0)
+    e_val = sig(S.activation(T.vals[:, 512:1024], T.vals[:, 0:512], Fn.Identity, bias=512.0))
+    sig(S.activation(T.vals[:, 1024:NC], T.vals[:, 0:NC - 1024], Fn.Identity, bias=1024.0), e_val)
+
+    g.wait_ge(T.sem.dtab, 48)
+    g.remote_dma_fused([_tr(topo, cores[d], R["tab"][d], T.sem.tabs, T.tabd[:], T.tabr[rank]) for d in pairs[:7]],
+                       local_sem=T.sem.loc)
+    nloc = sum(len(R["tab"][d]) for d in pairs[:7])
+    g.sem_inc(T.sem.tsent, 1)
+
+    Y.wait_ge(T.sem.dtab, 48)
+    Y.wait_ge(T.sem.tabs, sum(len(roads[q]["tab"][rank]) for q in range(len(cores)) if q != rank))
+    Y.dma_start(T.tab1[0:1, 0:16], T.tabr[:, 2 * rank:2 * rank + 2, 0]).then_inc(T.sem.dtw, 16)
+    g.wait_ge(T.sem.dtw, 16)
     e_pb = sig(g.partition_broadcast(T.tabb[:], T.tab1[0:1, 0:16], 128))
 
     need("V", e_pidx)
@@ -194,21 +169,11 @@ def rank_program(g, core, T, topo):
     sig(V.tensor_scalar(T.evf[:, 0:1], T.pi2[:, 0:1], -1.0, 1.0, Op.mult, Op.add), e_c)
     need("V", e_iot, e_p16)
     sig(V.tensor_scalar(T.dumpc[:], T.iot[:], T.p16f[:, 0:1], None, Op.add), e_c)
-    e_one = sig(V.memset(T.ones[:], 1.0))
     e_pz = sig(V.memset(T.posw[:, 0:512], 0.0))
-    need("V", e_pb)
-    e_tab = sig(V.tensor_scalar(T.tabf[:], T.tabb[:], 0.0, 512.0, Op.max, Op.mult))
-
-    need("g", e_tab)
-    g.remote_dma_fused([_tr(topo, cores[d], R["tab"][d], T.sem.tabs, T.tabf[:, 2 * d:2 * d + 2],
-                            T.tabl[:, 2 * rank:2 * rank + 2]) for d in pairs[:7]], local_sem=T.sem.loc)
-    nloc = sum(len(R["tab"][d]) for d in pairs[:7])
-    g.sem_inc(T.sem.tsent, 1)
 
     V.wait_ge(T.sem.dt, 128)
     e_ox = sig(V.tensor_scalar(T.offx[:], T.tokS[:], 0.0, 4.0, Op.max, Op.mult))
-    need("V", e_one, e_c)
-    e_val = sig(V.tensor_tensor_scan(T.vals[:], T.ones[:], T.ones[:], float(W0 - 1), Op.mult, Op.add))
+    need("V", e_c)
     e3 = sig(V.tensor_scalar(T.tokA[:], T.tokS[:], T.odd16[:, 0:1], None, Op.subtract))
     e4 = sig(V.tensor_scalar(T.negf[:], T.tokS[:], 0.0, None, Op.is_lt))
     need("V", e3)
@@ -220,7 +185,13 @@ def rank_program(g, core, T, topo):
     need("V", e7)
     e8 = sig(V.tensor_copy(T.offs[:], T.offf[:]))
     need("V", e8, e_val, e_pz)
-    e_sc = sig(V.tensor_copy(T.posw[:].indirect(T.offs[:]), T.vals[:]))
+    e_sc = new()
+
+    def scatter(a, b):
+        if a < b:
+            sig(V.tensor_copy(T.posw[:].indirect(T.offs[:, a // 16:b // 16]), T.vals[:, a:b]), e_sc)
+
+    scatter(0, SE)
     V.wait_ge(T.sem.dx, 16)
     e_xq = sig(V.quantize_mx(T.xc[:], T.xcs[:], T.xs[:]))
 
@@ -231,19 +202,24 @@ def rank_program(g, core, T, topo):
 
     S.wait_ge(T.sem.dx, 16)
     need("S", e_ox)
-    for t in range(3):
+    for t in range(XE):
         xgather(t)
 
-    V.wait_ge(T.sem.tabs, sum(len(roads[q]["tab"][rank]) for q in range(len(cores)) if q != rank))
-    e_off = []
-    for i, d in enumerate(pairs):
-        t, e = (T.tabf if d == rank else T.tabl), new()
-        for j in range(2):
-            sig(V.tensor_scalar(T.offa[:, 64 * i + 32 * j:64 * i + 32 * j + 32], T.dumpc[:, 0:32],
-                                t[:, 2 * (rank if d == rank else d) + j:2 * (rank if d == rank else d) + j + 1]
-                                if d != rank else t[:, 2 * rank + j:2 * rank + j + 1], -17.0, Op.add, Op.add), e)
-        e_off.append(e)
+    need("V", e_pb)
+    e_tab = sig(V.tensor_scalar(T.tabf[:], T.tabb[:], 0.0, 512.0, Op.max, Op.mult))
+    need("V", e_tab)
+    e_off = {}
 
+    def offsets(i):
+        if i < 8:
+            d, e = pairs[i], new()
+            for j in range(2):
+                sig(V.tensor_scalar(T.offa[:, 64 * i + 32 * j:64 * i + 32 * j + 32], T.dumpc[:, 0:32],
+                                    T.tabf[:, 2 * d + j:2 * d + j + 1], -17.0, Op.add, Op.add), e)
+            e_off[i] = e
+
+    offsets(0)
+    offsets(1)
     V.wait_ge(T.sem.dw, 128)
     S.wait_ge(T.sem.dw, 128)
     e_q = []
@@ -253,32 +229,29 @@ def rank_program(g, core, T, topo):
         es = sig(S.activation(T.ga[:, a:a + SPLIT], T.win[:].indirect(T.offa[:, 64 * i:64 * i + m]), Fn.Copy))
         need("V", e_off[i])
         ev = sig(V.tensor_copy(T.ga[:, a + SPLIT:a + 1024], T.win[:].indirect(T.offa[:, 64 * i + m:64 * i + 64])))
+        offsets(i + 2)
         need("V", es, ev)
         e_q.append(sig(V.quantize_mx(T.qc[:, 256 * i:256 * i + 256], T.qs[:, 256 * i:256 * i + 256], T.ga[:, a:a + 1024])))
-    xgather(3)
+    for t in range(XE, 4):
+        xgather(t)
+    scatter(SE, NC)
 
-    def send(items):
-        n = 0
-        for c, (b, l) in ((True, ("qc", "lc")), (False, ("qs", "ls"))):
-            ts = []
-            for i, w, dst, engines, sem, at in items:
-                src = _codes(T[b], 256 * i, 256 * i + w) if c else T[b][:, 256 * i:256 * i + w]
-                to = _codes(T[l], at, at + w) if c else T[l][:, at:at + w]
-                ts.append(_tr(topo, dst, engines, sem, src, to))
-                n += len(engines)
-            g.remote_dma_fused(ts, local_sem=T.sem.loc)
-        return n
+    bufs, held = (("qc", "lc"), ("qs", "ls")), {}
 
-    mine = T.sem["a%d" % rank]
-    need("g", e_q[0], e_q[1])
-    nloc += send([(0, 512, R["helper"], topo.engines(core, R["helper"]), T.sem.ha, 0)])
-    need("g", e_q[2], e_q[3])
-    nloc += send([(2, 256, R["helper"], R["on"], T.sem.hb, 512),
-                  (3, 256, cores[R["dir"][0]], R["eng"][R["dir"][0]], mine, 256 * rank)])
-    need("g", e_q[4], e_q[5])
-    nloc += send([(i, 256, cores[R["dir"][i - 3]], R["eng"][R["dir"][i - 3]], mine, 256 * rank) for i in (4, 5)])
-    need("g", e_q[6])
-    nloc += send([(6, 256, cores[R["nb"]], R["eng"][R["nb"]], mine, 256 * rank)])
+    def item(i):
+        d = pairs[i]
+        c = R["via"].get(d)
+        if c is None:
+            return (256 * i, 256, cores[d], R["eng"][d], T.sem["a%d" % rank], 256 * rank)
+        held[c] = held.get(c, -1) + 1
+        return (256 * i, 256, c, R["on"], T.sem["h%d" % held[c]], 256 * held[c])
+
+    for group in ((0, 1), (2, 3), (4, 5), (6,)):
+        need("g", *[e_q[i] for i in group])
+        items = [item(i) for i in group]
+        if group == (0, 1):
+            items = [it[:3] + (es,) + it[4:] for it, es in zip(items, (R["off"], R["on"]))]
+        nloc += _send(g, T, topo, bufs, items)
     g.wait_ge(T.sem.loc, nloc)
 
     need("V", e_sc)
@@ -308,10 +281,8 @@ def rank_program(g, core, T, topo):
     for a, b in ((0, 512), (512, 1024), (1024, NC)):
         e_gq.append(sig(V.quantize_mx(T.xgc[:, a:b], T.xgs[:, a:b], T.xg[:, 4 * a:4 * b])))
 
-    k, h, mem = R["k"], R["h"], R["mem"]
-    order = [rank, R["nb"], mem[k ^ 1][1 - h], mem[k ^ 1][h], mem[k ^ 2][1 - h], mem[k ^ 3][1 - h], mem[k ^ 2][h], mem[k ^ 3][h]]
     copies, n = [], 0
-    for src in order:
+    for src in R["order"]:
         if src == rank:
             need("P", e_q[7])
             cb, sb, at = T.qc, T.qs, 256 * 7

from concourse.bass import DstId, RemoteDMATransfer
from concourse.mybir import dt, AluOpType as Op, ActivationFunctionType as Fn

NB = 10
NC = 128 * NB
NAT = 6
W0 = 512 * NAT
SPLIT = 640
XE = 2
SE = 960
PW = 1824

SCRATCH = {n: ("sbuf", [128, w], d) for d, ws in {
    "int32": {"tab1": 16, "tabb": 16, "tokS": 80, "adS": 32, "pidx": 4, "pi1": 4, "pi2": 4, "tokA": 80, "tokB": 80},
    "bfloat16": {"tabf": 16, "win": 4096, "xs": 2048, "xg": 4 * NC, "ga": 8192},
    "uint16": {"offa": 512, "offx": 80, "offs": 80, "offy": 32},
    "float32": {"p16f": 4, "oddf": 4, "evf": 4, "odd16": 4, "iot": 80, "dumpc": 80, "negf": 80, "ndf": 80, "offf": 80,
                "vals": NC, "posw": PW, "trp": 512, "f1": 32, "f2": 32, "f3": 32, "n1": 32, "n2": 32, "n3": 32, "n4": 32,
                "tot": 32, "resw": W0 + NC, "ysb": 512},
    "float8_e4m3fn_x4": {"qc": 2048, "lc": 2048, "xc": 512, "xgc": NC},
    "uint8": {"qs": 2048, "ls": 2048, "xcs": 512, "xgs": NC},
}.items() for n, w in ws.items()}
SCRATCH["tabd"] = ("dram", [128, 1], "int32")
SCRATCH["tabr"] = ("dram", [8, 128, 1], "int32")
for _b in range(8):
    SCRATCH["ps%d" % _b] = ("psum", [128, 512], "float32")
SEMAPHORES = (["e%d" % _i for _i in range(120)] + ["a%d" % _i for _i in range(8)]
              + ["dtab", "dtw", "dx", "dw", "dt", "da", "dy0", "dy1", "tabs", "tsent", "loc", "h0", "h1"])


def _mask(es):
    return sum(1 << e for e in es)


def _road(r, T, topo):
    cores = list(T.cores)
    chips = []
    for c in cores:
        if topo.chip(c) not in chips:
            chips.append(topo.chip(c))
    mem = [[q for q in range(len(cores)) if topo.chip(cores[q]) == ch] for ch in chips]
    me = cores[r]
    k = chips.index(topo.chip(me))
    h = mem[k].index(r)
    rel = [mem[k ^ s][1 - h] for s in (1, 2, 3)]
    dire = [mem[k ^ s][h] for s in (1, 2, 3)]
    nb = mem[k][1 - h]
    free = [c for c in topo.cores_of(me) if c not in cores]
    port = [c for c in free if topo.die(c) != topo.die(me) and all(topo.may_write(c, cores[d]) for d in rel)]
    far = [c for c in free if topo.die(c) != topo.die(me) and c not in port and topo.may_write(c, cores[rel[1]])]
    near = [c for c in free if topo.die(c) == topo.die(me) and topo.may_write(c, cores[dire[1]])]
    via = {rel[0]: port[h], rel[2]: port[h], rel[1]: far[h], dire[1]: near[h]}
    off = topo.engines(me, cores[dire[0]])
    on = [e for e in topo.engines(me, cores[nb]) if e not in off]
    eng = {d: topo.engines(via.get(d, me), cores[d]) for d in rel + dire}
    eng[nb] = on
    tabe, left = {}, list(off)
    for i, d in enumerate(rel + dire):
        n = 2 if i < len(off) - len(rel + dire) else 1
        tabe[d], left = left[:n], left[n:]
    tabe[nb] = on
    pairs = [rel[0], rel[1], dire[1], dire[0], rel[2], dire[2], nb, r]
    return {"k": k, "h": h, "nb": nb, "via": via, "off": off, "on": on, "eng": eng, "tab": tabe, "pairs": pairs,
            "order": [r, nb, rel[0], rel[1], dire[0], dire[1], rel[2], dire[2]]}


def _tr(topo, dst, engines, sem, src, to):
    rid, pid, _se = topo.addr(dst)
    return RemoteDMATransfer(dst_ids=[DstId(rid=rid, pnc=pid)], dma_engine_mask=_mask(engines), remote_sem=sem, src=src, dst=to)


def _send(g, T, topo, bufs, items):
    n = 0
    for c, (b, l) in zip((True, False), bufs):
        ts = []
        for a, w, dst, engines, sem, at in items:
            src, to = T[b][:, a:a + w], T[l][:, at:at + w]
            ts.append(_tr(topo, dst, engines, sem, src.bitcast(dt.uint8) if c else src, to.bitcast(dt.uint8) if c else to))
            n += len(engines)
        g.remote_dma_fused(ts, local_sem=T.sem.loc)
    return n


def _relay(g, core, r, R, T, topo):
    n, i = 0, 0
    for d in R["pairs"]:
        if R["via"].get(d) == core:
            g.wait_ge(T.sem["h%d" % i], 2 * len(R["on"]))
            n += _send(g, T, topo, (("lc", "lc"), ("ls", "ls")),
                       [(256 * i, 256, T.cores[d], R["eng"][d], T.sem["a%d" % r], 256 * r)])
            i += 1
    g.wait_ge(T.sem.loc, n)


def rank_program(g, core, T, topo):
    rank = T.rank_of(core)
    cores = list(T.cores)
    roads = [_road(q, T, topo) for q in range(len(cores))]
    if rank is None:
        for q, R in enumerate(roads):
            if core in R["via"].values():
                _relay(g, core, q, R, T, topo)
        return
    R = roads[rank]
    V, S, P, Y = g.vector, g.scalar, g.tensor, g.sync
    pairs = R["pairs"]
    nat0 = 0 if R["k"] < 2 else 16 - NAT
    listed = [s for s in range(16) if not nat0 <= s < nat0 + NAT]
    c0 = 8 * listed[0]
    used = [0]
    waited = {}

    def new():
        used[0] += 1
        return ["e%d" % (used[0] - 1), 0]

    def sig(inst, e=None):
        e = e or new()
        inst.then_inc(T.sem[e[0]], 1)
        e[1] += 1
        return e

    def need(qn, *es):
        q = {"g": g, "V": V, "S": S, "P": P, "Y": Y}[qn]
        for e in es:
            if waited.get((qn, e[0]), 0) < e[1]:
                q.wait_ge(T.sem[e[0]], e[1])
                waited[(qn, e[0])] = e[1]

    Y.dma_start(T.tabd[0:16, :], T.tab[:]).then_inc(T.sem.dtab, 16)
    S.dma_start(T.tabd[16:128, :], T.tok[0:7, 0:16]).then_inc(T.sem.dtab, 16)
    S.dma_start(T.tabr[rank, 0:16, :], T.tab[:]).then_inc(T.sem.dtab, 16)
    for b in range(8):
        (S if b < 4 else Y).dma_start(T.tokS[16 * b:16 * b + 16, :], T.tok[:, c0:c0 + 80]).then_inc(T.sem.dt, 16)
    Y.dma_start(T.xs[:], T.x[:]).then_inc(T.sem.dx, 16)
    for m in range(8):
        if m == 4:
            Y.wait_ge(T.sem.tsent, 1)
        Y.dma_start(T.win[:, 512 * m:512 * m + 512], T.wa[128 * m:128 * m + 128, :]).then_inc(T.sem.dw, 16)
    for b in range(8):
        Y.dma_start(T.adS[16 * b:16 * b + 16, :], T.ad[:]).then_inc(T.sem.da, 16)

    e_pidx = sig(g.iota(T.pidx[:, 0:1], [[0, 1]], 0, 1))
    e_iot = sig(g.iota(T.iot[:], [[16, 80]], 17, 0, allow_small_or_imprecise_dtypes=True))
    e_v0 = sig(g.iota(T.vals[:, 0:512], [[1, 512]], W0, 0, allow_small_or_imprecise_dtypes=True))
    need("S", e_v0)
    e_val = sig(S.activation(T.vals[:, 512:1024], T.vals[:, 0:512], Fn.Identity, bias=512.0))
    sig(S.activation(T.vals[:, 1024:NC], T.vals[:, 0:NC - 1024], Fn.Identity, bias=1024.0), e_val)

    g.wait_ge(T.sem.dtab, 48)
    g.remote_dma_fused([_tr(topo, cores[d], R["tab"][d], T.sem.tabs, T.tabd[:], T.tabr[rank]) for d in pairs[:7]],
                       local_sem=T.sem.loc)
    nloc = sum(len(R["tab"][d]) for d in pairs[:7])
    g.sem_inc(T.sem.tsent, 1)

    Y.wait_ge(T.sem.dtab, 48)
    Y.wait_ge(T.sem.tabs, sum(len(roads[q]["tab"][rank]) for q in range(len(cores)) if q != rank))
    Y.dma_start(T.tab1[0:1, 0:16], T.tabr[:, 2 * rank:2 * rank + 2, 0]).then_inc(T.sem.dtw, 16)
    g.wait_ge(T.sem.dtw, 16)
    e_pb = sig(g.partition_broadcast(T.tabb[:], T.tab1[0:1, 0:16], 128))

    need("V", e_pidx)
    e1 = sig(V.tensor_scalar(T.pi1[:, 0:1], T.pidx[:, 0:1], 15, None, Op.bitwise_and))
    e2 = sig(V.tensor_scalar(T.pi2[:, 0:1], T.pidx[:, 0:1], 4, 1, Op.logical_shift_right, Op.bitwise_and))
    need("V", e1, e2)
    e_p16 = sig(V.tensor_copy(T.p16f[:, 0:1], T.pi1[:, 0:1]))
    e_c = sig(V.tensor_copy(T.oddf[:, 0:1], T.pi2[:, 0:1]))
    sig(V.tensor_scalar(T.odd16[:, 0:1], T.pi2[:, 0:1], 16.0, None, Op.mult), e_c)
    sig(V.tensor_scalar(T.evf[:, 0:1], T.pi2[:, 0:1], -1.0, 1.0, Op.mult, Op.add), e_c)
    need("V", e_iot, e_p16)
    sig(V.tensor_scalar(T.dumpc[:], T.iot[:], T.p16f[:, 0:1], None, Op.add), e_c)
    e_pz = sig(V.memset(T.posw[:, 0:512], 0.0))

    V.wait_ge(T.sem.dt, 128)
    e_ox = sig(V.tensor_scalar(T.offx[:], T.tokS[:], 0.0, 4.0, Op.max, Op.mult))
    need("V", e_c)
    e3 = sig(V.tensor_scalar(T.tokA[:], T.tokS[:], T.odd16[:, 0:1], None, Op.subtract))
    e4 = sig(V.tensor_scalar(T.negf[:], T.tokS[:], 0.0, None, Op.is_lt))
    need("V", e3)
    e5 = sig(V.tensor_scalar(T.tokB[:], T.tokA[:], 511, None, Op.bitwise_and))
    need("V", e4)
    e6 = sig(V.tensor_tensor(T.ndf[:], T.negf[:], T.dumpc[:], Op.mult))
    need("V", e5, e6)
    e7 = sig(V.tensor_tensor(T.offf[:], T.ndf[:], T.tokB[:], Op.add))
    need("V", e7)
    e8 = sig(V.tensor_copy(T.offs[:], T.offf[:]))
    need("V", e8, e_val, e_pz)
    e_sc = new()

    def scatter(a, b):
        if a < b:
            sig(V.tensor_copy(T.posw[:].indirect(T.offs[:, a // 16:b // 16]), T.vals[:, a:b]), e_sc)

    scatter(0, SE)
    V.wait_ge(T.sem.dx, 16)
    e_xq = sig(V.quantize_mx(T.xc[:], T.xcs[:], T.xs[:]))

    e_xg = new()

    def xgather(t):
        sig(S.activation(T.xg[:, t:4 * NC:4], T.xs[:, t:2048].indirect(T.offx[:]), Fn.Copy), e_xg)

    S.wait_ge(T.sem.dx, 16)
    need("S", e_ox)
    for t in range(XE):
        xgather(t)

    need("V", e_pb)
    e_tab = sig(V.tensor_scalar(T.tabf[:], T.tabb[:], 0.0, 512.0, Op.max, Op.mult))
    need("V", e_tab)
    e_off = {}

    def offsets(i):
        if i < 8:
            d, e = pairs[i], new()
            for j in range(2):
                sig(V.tensor_scalar(T.offa[:, 64 * i + 32 * j:64 * i + 32 * j + 32], T.dumpc[:, 0:32],
                                    T.tabf[:, 2 * d + j:2 * d + j + 1], -17.0, Op.add, Op.add), e)
            e_off[i] = e

    offsets(0)
    offsets(1)
    V.wait_ge(T.sem.dw, 128)
    S.wait_ge(T.sem.dw, 128)
    e_q = []
    for i in range(8):
        a, m = 1024 * i, SPLIT // 16
        need("S", e_off[i])
        es = sig(S.activation(T.ga[:, a:a + SPLIT], T.win[:].indirect(T.offa[:, 64 * i:64 * i + m]), Fn.Copy))
        need("V", e_off[i])
        ev = sig(V.tensor_copy(T.ga[:, a + SPLIT:a + 1024], T.win[:].indirect(T.offa[:, 64 * i + m:64 * i + 64])))
        offsets(i + 2)
        need("V", es, ev)
        e_q.append(sig(V.quantize_mx(T.qc[:, 256 * i:256 * i + 256], T.qs[:, 256 * i:256 * i + 256], T.ga[:, a:a + 1024])))
    for t in range(XE, 4):
        xgather(t)
    scatter(SE, NC)

    bufs, held = (("qc", "lc"), ("qs", "ls")), {}

    def item(i):
        d = pairs[i]
        c = R["via"].get(d)
        if c is None:
            return (256 * i, 256, cores[d], R["eng"][d], T.sem["a%d" % rank], 256 * rank)
        held[c] = held.get(c, -1) + 1
        return (256 * i, 256, c, R["on"], T.sem["h%d" % held[c]], 256 * held[c])

    for group in ((0, 1), (2, 3), (4, 5), (6,)):
        need("g", *[e_q[i] for i in group])
        items = [item(i) for i in group]
        if group == (0, 1):
            items = [it[:3] + (es,) + it[4:] for it, es in zip(items, (R["off"], R["on"]))]
        nloc += _send(g, T, topo, bufs, items)
    g.wait_ge(T.sem.loc, nloc)

    need("V", e_sc)
    e_t = sig(V.transpose(T.trp[:], T.posw[:, 0:512]))
    V.wait_ge(T.sem.da, 128)
    if nat0 == 0:
        n1 = sig(V.tensor_scalar(T.n1[:], T.adS[:], NAT - 0.5, None, Op.is_lt))
    else:
        n1 = sig(V.tensor_scalar(T.n1[:], T.adS[:], nat0 - 0.5, None, Op.is_gt))
    n2 = sig(V.tensor_scalar(T.n2[:], T.adS[:], 512.0, -512.0 * nat0 - 17.0, Op.mult, Op.add))
    need("V", e_t)
    f = sig(V.tensor_scalar(T.f1[:], T.trp[:, 0:512:16], T.evf[:, 0:1], None, Op.mult))
    sig(V.tensor_scalar(T.f2[:, 1:32], T.trp[:, 0:496:16], T.oddf[:, 0:1], None, Op.mult), f)
    sig(V.tensor_scalar(T.f2[:, 0:1], T.trp[:, 496:497], T.oddf[:, 0:1], None, Op.mult), f)
    need("V", n2)
    n3 = sig(V.tensor_tensor(T.n3[:], T.n2[:], T.dumpc[:, 0:32], Op.add))
    need("V", f)
    f3 = sig(V.tensor_tensor(T.f3[:], T.f1[:], T.f2[:], Op.add))
    need("V", n1, n3)
    n4 = sig(V.tensor_tensor(T.n4[:], T.n3[:], T.n1[:], Op.mult))
    need("V", n4, f3)
    tt = sig(V.tensor_tensor(T.tot[:], T.n4[:], T.f3[:], Op.add))
    need("V", tt)
    e_oy = sig(V.tensor_copy(T.offy[:], T.tot[:]))
    need("V", e_xg)
    e_gq = []
    for a, b in ((0, 512), (512, 1024), (1024, NC)):
        e_gq.append(sig(V.quantize_mx(T.xgc[:, a:b], T.xgs[:, a:b], T.xg[:, 4 * a:4 * b])))

    copies, n = [], 0
    for src in R["order"]:
        if src == rank:
            need("P", e_q[7])
            cb, sb, at = T.qc, T.qs, 256 * 7
        else:
            P.wait_ge(T.sem["a%d" % src], 2 * len(roads[src]["eng"][rank]))
            cb, sb, at = T.lc, T.ls, 256 * src
        for j in range(2):
            s, b = 2 * src + j, T["ps%d" % (n % 8)]
            if n >= 8:
                need("P", copies[n - 8])
            if s in listed:
                x0, w, xa, xb = 128 * listed.index(s), 128, T.xgc, T.xgs
                need("P", e_gq[x0 // 512])
                out = W0 + x0
            else:
                x0, w, xa, xb = 0, 512, T.xc, T.xcs
                need("P", e_xq)
                out = 512 * (s - nat0)
            e = sig(P.matmul_mx(b[:, 0:w], cb[:, at + 128 * j:at + 128 * j + 128], sb[:, at + 128 * j:at + 128 * j + 128],
                                xa[:, x0:x0 + w], xb[:, x0:x0 + w], True, True))
            if j == 0:
                need("S", e)
                copies.append(sig(S.activation(T.resw[:, out:out + w], b[:, 0:w], Fn.Copy)))
            else:
                need("V", e)
                copies.append(sig(V.tensor_copy(T.resw[:, out:out + w], b[:, 0:w])))
            n += 1

    need("V", e_oy, *copies)
    e_y = sig(V.tensor_copy(T.ysb[:, 0:256], T.resw[:].indirect(T.offy[:, 0:16])))
    need("S", e_oy, *copies)
    e_z = sig(S.activation(T.ysb[:, 256:512], T.resw[:].indirect(T.offy[:, 16:32]), Fn.Copy))
    need("Y", e_y)
    Y.dma_start(T.y[:, 0:256], T.ysb[:, 0:256]).then_inc(T.sem.dy0, 16)
    need("S", e_z)
    S.dma_start(T.y[:, 256:512], T.ysb[:, 256:512]).then_inc(T.sem.dy1, 16)
    Y.wait_ge(T.sem.dy0, 16)
    S.wait_ge(T.sem.dy1, 16)
